import numpy as np
import ml_dtypes


def mxq(x, axis, fmt="e4m3"):
    dtype, down = {"e4m3": (ml_dtypes.float8_e4m3fn, 7), "e5m2": (ml_dtypes.float8_e5m2, 14)}[fmt]
    v = np.moveaxis(np.asarray(x, np.float32).astype(ml_dtypes.bfloat16).astype(np.float64), axis, -1)
    blocks = v.reshape(v.shape[:-1] + (-1, 32))
    amax = np.abs(blocks).max(-1, keepdims=True)
    byte = np.maximum(np.where(amax > 0, np.frexp(amax)[1] - 1 + 127, 0) - down, 1)
    scale = np.exp2(byte - 127.0)
    codes = (blocks / scale).astype(np.float32).astype(dtype).astype(np.float64)
    return np.moveaxis((codes * scale).reshape(v.shape), -1, axis)


WIDE = False


def mx_kscale(k):
    if not WIDE:
        return np.ones(k)
    levels = np.array([10, -10, 5, -5, 0])
    if k % 512:
        return np.exp2(np.random.permutation(np.resize(levels, k // 32))).repeat(32)
    a = np.empty((k // 512, 16))
    for p in range(k // 512):
        a[p, :8] = np.random.permutation(np.resize(levels, 8))
        for g in range(8):
            far = levels[np.abs(levels - a[p, g]) >= 10]
            a[p, g + 8] = far[np.random.randint(len(far))]
    return np.exp2(a.ravel()).repeat(32)


def f64(x):
    return np.asarray(x).astype(np.float64)


def striped(idx):
    return np.tile(idx.reshape(-1, 16).T, (8, 1)).astype(np.uint16)


def unstriped(offs):
    return offs[:16].T.reshape(-1).astype(np.int64)


E2M1 = np.array([0.0, 0.5, 1.0, 1.5, 2.0, 3.0, 4.0, 6.0, -0.0, -0.5, -1.0, -1.5, -2.0, -3.0, -4.0, -6.0])


def pack_weight(w, fmt):
    k, n = w.shape
    w = f64(np.asarray(w, np.float32).astype(ml_dtypes.bfloat16)).reshape(k // 32, 32, n)
    amax = np.abs(w).max(1)
    if fmt == "e4m3":
        byte = np.frexp(amax)[1] - 1 + 127 - 7
    else:
        mant, ex = np.frexp(amax / 6.0)
        byte = np.where(mant > 0.5, ex, ex - 1) + 127
    byte = np.clip(np.where(amax > 0, byte, 1), 1, 254)
    scaled = (w * np.exp2(127.0 - byte)[:, None, :]).reshape(k, n).astype(np.float32)
    by_word = np.ascontiguousarray(scaled.reshape(k // 512, 128, 4, n).transpose(0, 1, 3, 2))
    if fmt == "e4m3":
        words = by_word.astype(ml_dtypes.float8_e4m3fn).view(np.uint8)
    else:
        c = by_word.astype(ml_dtypes.float4_e2m1fn).view(np.uint8) & 0xF
        words = (c[..., 0::2] | (c[..., 1::2] << 4)).reshape(k // 512, 128, 2 * n)
    return np.ascontiguousarray(words), np.ascontiguousarray(byte.astype(np.uint8).reshape(k // 512, 16, n))


def unpack_weight(words, scales, fmt):
    g, _, n = scales.shape
    words = np.ascontiguousarray(words).reshape(g, 128, n, -1)
    if fmt == "e4m3":
        vals = words.view(ml_dtypes.float8_e4m3fn).astype(np.float64)
    else:
        nib = np.empty((g, 128, n, 4), np.uint8)
        nib[..., 0::2] = words & 0xF
        nib[..., 1::2] = words >> 4
        vals = E2M1[nib]
    vals = vals * np.repeat(np.exp2(scales.astype(np.float64) - 127.0), 8, axis=1)[..., None]
    return vals.transpose(0, 1, 3, 2).reshape(g * 512, n)


def relu(v):
    return np.maximum(v, 0.0)


K, T, Q, E, C, D, H = 1024, 512, 1024, 4, 128, 256, 512
N = 512


def by_expert(wq, xq, C):
    return np.concatenate([wq[e].T @ xq[:, e * C:(e + 1) * C] for e in range(E)], axis=1)


def setup_inputs():
    n = np.random.standard_normal
    s = mx_kscale(K)
    u = mx_kscale(H)
    slot_token = np.random.permutation(T)[:E * C]
    slots2 = np.concatenate([np.random.permutation(Q)[:D] for e in range(E)])
    x = pack_weight(n((K, Q)) * s[:, None], "e4m3")
    return {
        "x_words": x[0],
        "x_scales": x[1],
        "xo": (n((K, T)) * s[:, None]).astype(np.float32),
        "w1": (n((E, K, H)) / np.sqrt(K) / s[None, :, None] * u).astype(np.float32),
        "w2": (n((E, H, N)) / np.sqrt(H) / u[None, :, None]).astype(np.float32),
        "gate": np.tile(np.random.uniform(0.2, 1.0, E * C), (128, 1)).astype(np.float32),
        "offs": striped(slot_token),
        "offs2": striped(slots2),
    }


def reference(x_words, x_scales, xo, w1, w2, gate, offs, offs2):
    w1q = mxq(f64(w1), 1, "e4m3")
    w2q = mxq(f64(w2), 1, "e4m3")
    idx, idx2 = unstriped(offs), unstriped(offs2)
    xq = mxq(f64(xo)[:, idx], 0, "e4m3")
    rq = unpack_weight(x_words, x_scales, "e4m3")[:, idx2]
    h = relu(by_expert(w1q, xq, C))
    y = by_expert(w2q, mxq(h, 0, "e4m3"), C)
    h = relu(by_expert(w1q, rq, D))
    z = by_expert(w2q, mxq(h, 0, "e4m3"), D)
    own = np.zeros((N, T))
    own[:, idx] = f64(gate[:1]) * y
    return np.concatenate([own, z], axis=1)

@@ -1,0 +1,260 @@
+from contextlib import ExitStack
+
+import concourse.mybir as mybir
+
+K, T, Q, E, C, D, H, N = 1024, 512, 1024, 4, 128, 256, 512, 512
+FLOPS = 2 * E * (C + D) * (K * H + H * N)
+
+F32 = mybir.dt.float32
+BF16 = mybir.dt.bfloat16
+I32 = mybir.dt.int32
+U32 = mybir.dt.uint32
+U16 = mybir.dt.uint16
+U8 = mybir.dt.uint8
+FP8X4 = mybir.dt.float8_e4m3fn_x4
+RELU = mybir.ActivationFunctionType.Relu
+MULT = mybir.AluOpType.mult
+ADD = mybir.AluOpType.add
+
+P = 128
+PASSES = K // 512
+LOADS = ["xw1","l2","sc","xw0","xo11","xo10","xo00","xo01","l1","w100","w101","w20","w110","w111","gate","w121","w22","w120","w21","w130","w131","w230","w231"]
+WHO = {"w22":"B","w131":"V","w111":"B","w120":"V"}
+STEPS = [["cx",1,0],["cx",1,1],["cx",0,0],["cx",0,1],["go",1],["go",0],["p1",0,0],["gf",0],["gf",1],["p1",0,1],["gf",2],["o1",0],["p2",0],["gf",3],["o2",0],["f1",0],["p1",1,0],["go",2],["p1",1,1],["o1",1],["f2",0],["go",3],["p1",2,1],["p1",2,0],["p2",2],["f1",1],["f1",2],["p2",1],["p1",3,1],["o1",2],["p1",3,0],["o2",1],["p2",3],["f1",3],["o1",3],["f2",3],["o2",2],["f2",1],["f2",2],["o2",3]]
+SPLIT = [3]
+BUFS = {"raw":9,"w":3,"hb":3,"ob":5,"hf":3,"ho":1,"sums":2}
+OWN_PARTS = 4
+GATE_IN_SCATTER = True
+
+
+def tile_moe_loc_mlp_relu_kernel(tc, x_words, x_scales, xo, w1, w2, gate, offs, offs2, out):
+    nc = tc.nc
+    with ExitStack() as ctx:
+        keep = ctx.enter_context(tc.tile_pool(name="keep", bufs=1))
+        psum = ctx.enter_context(tc.psum_pool(name="psum", bufs=1))
+
+        def held(shape, dtype, name):
+            return keep.tile(shape, dtype, name=name, align_bytes=64)
+
+        own_list = held([P, T // 16], U16, "own_list")
+        far_list = held([P, E * D // 16], U16, "far_list")
+        far_words = [held([P, Q], I32, f"far_words{s}") for s in range(PASSES)]
+        far_bytes = held([P, Q // 4], I32, "far_bytes")
+        rings = {
+            "raw": [held([P, 4 * H], F32, f"raw{i}") for i in range(BUFS["raw"])],
+            "w": [held([P, 4 * H], BF16, f"w_bf{i}") for i in range(BUFS["w"])],
+            "hf": [held([P, 4 * D], BF16, f"hidden_far{i}") for i in range(BUFS["hf"])],
+            "ho": [held([P, 4 * C], BF16, f"hidden_own{i}") for i in range(BUFS["ho"])],
+            "sums": [held([P, 4 * C], F32, f"sums{i}") for i in range(BUFS["sums"])],
+            "hb": [psum.tile([P, 512], F32, name=f"h_bank{i}") for i in range(BUFS["hb"])],
+            "ob": [psum.tile([P, 512], F32, name=f"o_bank{i}") for i in range(BUFS["ob"])],
+        }
+        taken = {name: 0 for name in rings}
+
+        def take(name):
+            taken[name] += 1
+            return rings[name][(taken[name] - 1) % BUFS[name]]
+
+        w_raw = {}
+        pending = list(LOADS)
+        staged = []
+        rounded = set()
+        gates = held([P, E * C], F32, "gates")
+
+        nc.vector.memset(far_bytes[:], 0)
+        scale_rows = x_scales.bitcast(I32)
+
+        def load(name):
+            if name == "sc":
+                for q in range(4):
+                    nc.scalar.dma_start(out=far_bytes[32 * q : 32 * q + 8, :], in_=scale_rows[:, 4 * q : 4 * q + 4, :])
+            elif name == "l1":
+                nc.sync.dma_start(own_list[:], offs)
+            elif name == "l2":
+                nc.sync.dma_start(far_list[:], offs2)
+            elif name == "gate":
+                nc.sync.dma_start(out=gates[:], in_=gate)
+            elif name.startswith("xw"):
+                s = int(name[2])
+                nc.sync.dma_start(out=far_words[s][:], in_=x_words[s].rearrange("p t d -> p (t d)").bitcast(I32))
+            else:
+                if name.startswith("xo"):
+                    s, u = int(name[2]), int(name[3])
+                    rows = xo[512 * s : 512 * (s + 1), :].rearrange("(p j) t -> p j t", j=4)[:, 2 * u : 2 * u + 2, :]
+                elif name.startswith("w1"):
+                    e, s = int(name[2]), int(name[3])
+                    rows = w1[e, 512 * s : 512 * (s + 1), :].rearrange("(p j) c -> p j c", j=4)
+                elif len(name) == 3:
+                    rows = w2[int(name[2])].rearrange("(p j) n -> p j n", j=4)
+                else:
+                    h = int(name[3])
+                    rows = w2[int(name[2])][:, 256 * h : 256 * (h + 1)].rearrange("(p j) n -> p j n", j=4)
+                j, width = rows.shape[1], rows.shape[2]
+                w_raw[name] = take("raw")[:, : j * width].rearrange("p (j c) -> p j c", j=j)
+                nc.sync.dma_start(out=w_raw[name], in_=rows)
+
+        def load_ahead():
+            while pending:
+                name = pending[0]
+                if name[0] == "w" or name.startswith("xo"):
+                    if len(staged) >= BUFS["raw"] and staged[-BUFS["raw"]] not in rounded:
+                        return
+                    staged.append(name)
+                load(pending.pop(0))
+
+        xo_pairs = [[held([P, T, 2], BF16, f"xo_pairs{s}{u}") for u in range(2)] for s in range(PASSES)]
+        own_bf = [[held([P, 4 * T // OWN_PARTS], BF16, f"own_bf{s}{a}") for a in range(OWN_PARTS)] for s in range(PASSES)]
+        own_codes = [[held([P, T // OWN_PARTS], U32, f"own_codes{s}{a}") for a in range(OWN_PARTS)] for s in range(PASSES)]
+        own_scales = [[held([P, T // OWN_PARTS], U8, f"own_scales{s}{a}") for a in range(OWN_PARTS)] for s in range(PASSES)]
+        far_codes = [[held([P, D], U32, f"far_codes{e}{s}") for s in range(PASSES)] for e in range(E)]
+        far_scales = [held([P, D], U8, f"far_scales{e}") for e in range(E)]
+        w1_codes = [[held([P, H], U32, f"w1_codes{e}{s}") for s in range(PASSES)] for e in range(E)]
+        w1_scales = [[held([P, H], U8, f"w1_scales{e}{s}") for s in range(PASSES)] for e in range(E)]
+        w2_codes = [held([P, N], U32, f"w2_codes{e}") for e in range(E)]
+        w2_scales = [held([P, N], U8, f"w2_scales{e}") for e in range(E)]
+        hf_codes = [held([P, D], U32, f"hf_codes{e}") for e in range(E)]
+        hf_scales = [held([P, D], U8, f"hf_scales{e}") for e in range(E)]
+        ho_codes = [held([P, C], U32, f"ho_codes{e}") for e in range(E)]
+        ho_scales = [held([P, C], U8, f"ho_scales{e}") for e in range(E)]
+        own_out = [held([P, T], F32, f"own_out{c}") for c in range(4)]
+        far_out = [held([P, 4, D], F32, f"far_out{e}") for e in range(E)]
+        scattered = []
+
+        def cast(name, dst, src):
+            who = WHO.get(name, "S")
+            rounded.add(name)
+            half = dst.shape[1] // 2
+            if who == "S":
+                nc.scalar.copy(out=dst, in_=src)
+            elif who == "V":
+                nc.vector.tensor_copy(out=dst, in_=src)
+            elif who == "G":
+                for a in range(4):
+                    part = slice(a * half // 2, (a + 1) * half // 2)
+                    nc.gpsimd.tensor_scalar(out=dst[:, part], in0=src[:, part], scalar1=1.0, scalar2=0.0, op0=MULT, op1=ADD)
+            else:
+                nc.scalar.copy(out=dst[:, :half], in_=src[:, :half])
+                nc.vector.tensor_copy(out=dst[:, half:], in_=src[:, half:])
+
+        def cast_xo(s, u):
+            cast(f"xo{s}{u}", xo_pairs[s][u][:], w_raw[f"xo{s}{u}"].rearrange("p r t -> p t r"))
+
+        def gather_own(a):
+            for s in range(PASSES):
+                words = own_bf[s][a][:].bitcast(U32).rearrange("p (n u) -> p n u", u=2)
+                for u in range(2):
+                    window = xo_pairs[s][u][:].rearrange("p t r -> p (t r)").bitcast(U32)
+                    nc.vector.tensor_copy(words[:, :, u], window.indirect(own_list[:, 32 // OWN_PARTS * a : 32 // OWN_PARTS * (a + 1)]))
+            for s in range(PASSES):
+                nc.vector.quantize_mx(out=own_codes[s][a][:].bitcast(FP8X4), scales=own_scales[s][a][:], in_=own_bf[s][a][:])
+
+        def gather_far(e):
+            slots = far_list[:, 16 * e : 16 * (e + 1)]
+            nc.vector.tensor_copy(far_codes[e][0][:], far_words[0][:].bitcast(U32).indirect(slots))
+            nc.vector.tensor_copy(far_scales[e][:], far_bytes[:].bitcast(U8).indirect(slots))
+            nc.vector.tensor_copy(far_codes[e][1][:], far_words[1][:].bitcast(U32).indirect(slots))
+
+        def prepare_w1(e, s):
+            grouped = take("w")
+            cast(
+                f"w1{e}{s}",
+                grouped[:].rearrange("p (t m j) -> p m j t", t=4, j=4),
+                w_raw[f"w1{e}{s}"].rearrange("p j (m t) -> p m j t", t=4),
+            )
+            nc.vector.quantize_mx(out=w1_codes[e][s][:].bitcast(FP8X4), scales=w1_scales[e][s][:], in_=grouped[:])
+
+        def prepare_w2(e):
+            parts = [(f"w2{e}{h}", slice(256 * h, 256 * (h + 1)), 256) for h in range(2)] if e in SPLIT else [(f"w2{e}", slice(0, N), N)]
+            for name, cols, width in parts:
+                grouped = take("w")[:, : 4 * width]
+                cast(
+                    name,
+                    grouped.rearrange("p (c i j) -> p c j i", i=4, j=4),
+                    w_raw[name].rearrange("p j (c i) -> p c j i", i=4),
+                )
+                nc.vector.quantize_mx(out=w2_codes[e][:, cols].bitcast(FP8X4), scales=w2_scales[e][:, cols], in_=grouped)
+
+        def first_bank(e, name, hidden, operands):
+            bank = take("hb")[:].rearrange("p (t n) -> p t n", t=4)
+            for t in range(4):
+                for s in range(PASSES):
+                    nc.tensor.matmul_mx(
+                        out=bank[:, t, :],
+                        lhsT=w1_codes[e][s][:, P * t : P * (t + 1)].bitcast(FP8X4),
+                        lhsT_scale=w1_scales[e][s][:, P * t : P * (t + 1)],
+                        rhs=operands[s][0].bitcast(FP8X4),
+                        rhs_scale=operands[s][1],
+                        start=(s == 0),
+                        stop=(s == PASSES - 1),
+                    )
+            dst, src = hidden.rearrange("p (n t) -> p n t", t=4), bank.rearrange("p t n -> p n t")
+            if WHO.get(name, "S") == "S":
+                nc.scalar.activation(out=dst, in_=src, func=RELU)
+            else:
+                nc.vector.tensor_scalar_max(out=dst, in0=src, scalar1=0.0)
+
+        def first_far(e):
+            hidden = take("hf")
+            for g in range(2):
+                cols = slice(P * g, P * (g + 1))
+                first_bank(e, f"hf{e}{g}", hidden[:, 512 * g : 512 * (g + 1)], [(far_codes[e][s][:, cols], far_scales[e][4 * s :, cols]) for s in range(PASSES)])
+            nc.vector.quantize_mx(out=hf_codes[e][:].bitcast(FP8X4), scales=hf_scales[e][:], in_=hidden[:])
+
+        def first_own(e):
+            hidden = take("ho")
+            a, b = divmod(e, E // OWN_PARTS)
+            cols = slice(C * b, C * (b + 1))
+            first_bank(e, f"ho{e}", hidden[:], [(own_codes[s][a][:, cols], own_scales[s][a][:, cols]) for s in range(PASSES)])
+            nc.vector.quantize_mx(out=ho_codes[e][:].bitcast(FP8X4), scales=ho_scales[e][:], in_=hidden[:])
+
+        def second_matmul(e, c, dst, codes, scales):
+            nc.tensor.matmul_mx(
+                out=dst,
+                lhsT=w2_codes[e][:, P * c : P * (c + 1)].bitcast(FP8X4),
+                lhsT_scale=w2_scales[e][:, P * c : P * (c + 1)],
+                rhs=codes[:].bitcast(FP8X4),
+                rhs_scale=scales[:],
+                start=True,
+                stop=True,
+            )
+
+        def second_far(e):
+            for b in range(2):
+                far_bank = take("ob")[:].rearrange("p (i m) -> p i m", i=2)
+                for i in range(2):
+                    second_matmul(e, 2 * b + i, far_bank[:, i, :], hf_codes[e], hf_scales[e])
+                if WHO.get(f"zf{e}{b}", "S") == "S":
+                    nc.scalar.copy(out=far_out[e][:, 2 * b : 2 * b + 2, :], in_=far_bank)
+                else:
+                    nc.vector.tensor_copy(out=far_out[e][:, 2 * b : 2 * b + 2, :], in_=far_bank)
+            nc.sync.dma_start(
+                out=out[:, T + D * e : T + D * (e + 1)].rearrange("(c p) m -> p c m", p=P), in_=far_out[e][:]
+            )
+
+        def second_own(e):
+            scattered.append(e)
+            slots = slice(C * e, C * (e + 1))
+            for tiles in ([(0, 1), (2, 3)] if e in SPLIT else [(0, 1, 2, 3)]):
+                n = len(tiles)
+                bank = take("ob")[:, : n * C].rearrange("p (i m) -> p i m", i=n)
+                for i, c in enumerate(tiles):
+                    second_matmul(e, c, bank[:, i, :], ho_codes[e], ho_scales[e])
+                sums = take("sums")[:, : n * C].rearrange("p (i m) -> p i m", i=n)
+                if GATE_IN_SCATTER:
+                    nc.scalar.copy(out=sums, in_=bank)
+                else:
+                    nc.vector.tensor_tensor(out=sums, in0=bank, in1=gates[:, slots].unsqueeze(1).broadcast_to([P, n, C]), op=MULT)
+                for i, c in enumerate(tiles):
+                    window = own_out[c][:].indirect(own_list[:, 8 * e : 8 * (e + 1)])
+                    if GATE_IN_SCATTER:
+                        nc.vector.tensor_tensor(window, sums[:, i, :], gates[:, slots], MULT)
+                    else:
+                        nc.vector.tensor_copy(window, sums[:, i, :])
+                    if len(scattered) == E:
+                        nc.sync.dma_start(out=out[P * c : P * (c + 1), 0:T], in_=own_out[c][:])
+
+        steps = {"cx": cast_xo, "gf": gather_far, "go": gather_own, "p1": prepare_w1, "p2": prepare_w2, "f1": first_far, "o1": first_own, "f2": second_far, "o2": second_own}
+        load_ahead()
+        for step in STEPS:
+            steps[step[0]](*step[1:])
+            load_ahead()

@@ -18,13 +18,14 @@ ADD = mybir.AluOpType.add
 
 P = 128
 PASSES = K // 512
-LOADS = ["xw1","l2","sc","xw0","xo11","xo10","xo00","xo01","l1","w100","w101","w20","w110","w111","gate","w121","w22","w120","w21","w130","w131","w230","w231"]
-WHO = {"w22":"B","w131":"V","w111":"B","w120":"V"}
-STEPS = [["cx",1,0],["cx",1,1],["cx",0,0],["cx",0,1],["go",1],["go",0],["p1",0,0],["gf",0],["gf",1],["p1",0,1],["gf",2],["o1",0],["p2",0],["gf",3],["o2",0],["f1",0],["p1",1,0],["go",2],["p1",1,1],["o1",1],["f2",0],["go",3],["p1",2,1],["p1",2,0],["p2",2],["f1",1],["f1",2],["p2",1],["p1",3,1],["o1",2],["p1",3,0],["o2",1],["p2",3],["f1",3],["o1",3],["f2",3],["o2",2],["f2",1],["f2",2],["o2",3]]
+LOADS = ["xw1","l2","xo00","sc","xo01","l1","xo10","w101","w100","xo11","xw0","w111","w20","w121","w21","w120","w110","w131","gate","w130","w22","w230","w231"]
+WHO = {"w231":"V","w130":"V","w111":"C","w120":"A","ho0":"V","w121":"C","w110":"C","hf00":"V","hf01":"V"}
+STEPS = [["cx",0,1],["cx",0,0],["p1",0,0],["p1",2,1],["cx",1,0],["p1",0,1],["p1",2,0],["cx",1,1],["go",3],["p1",1,1],["p2",1],["gf",0],["go",1],["go",0],["f1",0],["p1",1,0],["gf",1],["p2",0],["gf",2],["go",2],["p1",3,0],["o1",1],["o1",0],["o2",0],["p1",3,1],["f1",1],["p2",3],["o2",1],["p2",2],["f1",2],["gf",3],["f2",0],["o1",2],["o1",3],["f1",3],["o2",2],["f2",3],["f2",1],["f2",2],["o2",3]]
 SPLIT = [3]
-BUFS = {"raw":9,"w":3,"hb":3,"ob":5,"hf":3,"ho":1,"sums":2}
+BUFS = {"raw":7,"w":5,"hb":4,"ob":4,"hf":3,"ho":3,"sums":2,"fc":4,"oc":4,"og":4}
+Y_SPLIT = [0,1,2]
 OWN_PARTS = 4
-GATE_IN_SCATTER = True
+GATE_IN_SCATTER = False
 
 
 def tile_moe_loc_mlp_relu_kernel(tc, x_words, x_scales, xo, w1, w2, gate, offs, offs2, out):
@@ -46,6 +47,9 @@ def tile_moe_loc_mlp_relu_kernel(tc, x_words, x_scales, xo, w1, w2, gate, offs, 
             "hf": [held([P, 4 * D], BF16, f"hidden_far{i}") for i in range(BUFS["hf"])],
             "ho": [held([P, 4 * C], BF16, f"hidden_own{i}") for i in range(BUFS["ho"])],
             "sums": [held([P, 4 * C], F32, f"sums{i}") for i in range(BUFS["sums"])],
+            "og": [[held([P, 4 * T // OWN_PARTS], BF16, f"own_bf{i}{s}") for s in range(PASSES)] for i in range(min(BUFS["og"], OWN_PARTS))],
+            "oc": [[(held([P, T // OWN_PARTS], U32, f"own_codes{i}{s}"), held([P, T // OWN_PARTS], U8, f"own_scales{i}{s}")) for s in range(PASSES)] for i in range(min(BUFS["oc"], OWN_PARTS))],
+            "fc": [([held([P, D], U32, f"far_codes{i}{s}") for s in range(PASSES)], held([P, D], U8, f"far_scales{i}")) for i in range(BUFS["fc"])],
             "hb": [psum.tile([P, 512], F32, name=f"h_bank{i}") for i in range(BUFS["hb"])],
             "ob": [psum.tile([P, 512], F32, name=f"o_bank{i}") for i in range(BUFS["ob"])],
         }
@@ -61,13 +65,13 @@ def tile_moe_loc_mlp_relu_kernel(tc, x_words, x_scales, xo, w1, w2, gate, offs, 
         rounded = set()
         gates = held([P, E * C], F32, "gates")
 
-        nc.vector.memset(far_bytes[:], 0)
+        nc.gpsimd.memset(far_bytes[:], 0)
         scale_rows = x_scales.bitcast(I32)
 
         def load(name):
             if name == "sc":
                 for q in range(4):
-                    nc.scalar.dma_start(out=far_bytes[32 * q : 32 * q + 8, :], in_=scale_rows[:, 4 * q : 4 * q + 4, :])
+                    nc.sync.dma_start(out=far_bytes[32 * q : 32 * q + 8, :], in_=scale_rows[:, 4 * q : 4 * q + 4, :])
             elif name == "l1":
                 nc.sync.dma_start(own_list[:], offs)
             elif name == "l2":
@@ -103,11 +107,7 @@ def tile_moe_loc_mlp_relu_kernel(tc, x_words, x_scales, xo, w1, w2, gate, offs, 
                 load(pending.pop(0))
 
         xo_pairs = [[held([P, T, 2], BF16, f"xo_pairs{s}{u}") for u in range(2)] for s in range(PASSES)]
-        own_bf = [[held([P, 4 * T // OWN_PARTS], BF16, f"own_bf{s}{a}") for a in range(OWN_PARTS)] for s in range(PASSES)]
-        own_codes = [[held([P, T // OWN_PARTS], U32, f"own_codes{s}{a}") for a in range(OWN_PARTS)] for s in range(PASSES)]
-        own_scales = [[held([P, T // OWN_PARTS], U8, f"own_scales{s}{a}") for a in range(OWN_PARTS)] for s in range(PASSES)]
-        far_codes = [[held([P, D], U32, f"far_codes{e}{s}") for s in range(PASSES)] for e in range(E)]
-        far_scales = [held([P, D], U8, f"far_scales{e}") for e in range(E)]
+        own_codes, far_codes = {}, {}
         w1_codes = [[held([P, H], U32, f"w1_codes{e}{s}") for s in range(PASSES)] for e in range(E)]
         w1_scales = [[held([P, H], U8, f"w1_scales{e}{s}") for s in range(PASSES)] for e in range(E)]
         w2_codes = [held([P, N], U32, f"w2_codes{e}") for e in range(E)]
@@ -123,7 +123,7 @@ def tile_moe_loc_mlp_relu_kernel(tc, x_words, x_scales, xo, w1, w2, gate, offs, 
         def cast(name, dst, src):
             who = WHO.get(name, "S")
             rounded.add(name)
-            half = dst.shape[1] // 2
+            half = dst.shape[1] * {"A": 1, "C": 3}.get(who, 2) // 4
             if who == "S":
                 nc.scalar.copy(out=dst, in_=src)
             elif who == "V":
@@ -140,19 +140,21 @@ def tile_moe_loc_mlp_relu_kernel(tc, x_words, x_scales, xo, w1, w2, gate, offs, 
             cast(f"xo{s}{u}", xo_pairs[s][u][:], w_raw[f"xo{s}{u}"].rearrange("p r t -> p t r"))
 
         def gather_own(a):
+            own_bf, own_codes[a] = take("og"), take("oc")
             for s in range(PASSES):
-                words = own_bf[s][a][:].bitcast(U32).rearrange("p (n u) -> p n u", u=2)
+                words = own_bf[s][:].bitcast(U32).rearrange("p (n u) -> p n u", u=2)
                 for u in range(2):
                     window = xo_pairs[s][u][:].rearrange("p t r -> p (t r)").bitcast(U32)
                     nc.vector.tensor_copy(words[:, :, u], window.indirect(own_list[:, 32 // OWN_PARTS * a : 32 // OWN_PARTS * (a + 1)]))
             for s in range(PASSES):
-                nc.vector.quantize_mx(out=own_codes[s][a][:].bitcast(FP8X4), scales=own_scales[s][a][:], in_=own_bf[s][a][:])
+                nc.vector.quantize_mx(out=own_codes[a][s][0][:].bitcast(FP8X4), scales=own_codes[a][s][1][:], in_=own_bf[s][:])
 
         def gather_far(e):
+            far_codes[e] = take("fc")
             slots = far_list[:, 16 * e : 16 * (e + 1)]
-            nc.vector.tensor_copy(far_codes[e][0][:], far_words[0][:].bitcast(U32).indirect(slots))
-            nc.vector.tensor_copy(far_scales[e][:], far_bytes[:].bitcast(U8).indirect(slots))
-            nc.vector.tensor_copy(far_codes[e][1][:], far_words[1][:].bitcast(U32).indirect(slots))
+            nc.vector.tensor_copy(far_codes[e][0][0][:], far_words[0][:].bitcast(U32).indirect(slots))
+            nc.vector.tensor_copy(far_codes[e][1][:], far_bytes[:].bitcast(U8).indirect(slots))
+            nc.vector.tensor_copy(far_codes[e][0][1][:], far_words[1][:].bitcast(U32).indirect(slots))
 
         def prepare_w1(e, s):
             grouped = take("w")
@@ -197,14 +199,14 @@ def tile_moe_loc_mlp_relu_kernel(tc, x_words, x_scales, xo, w1, w2, gate, offs, 
             hidden = take("hf")
             for g in range(2):
                 cols = slice(P * g, P * (g + 1))
-                first_bank(e, f"hf{e}{g}", hidden[:, 512 * g : 512 * (g + 1)], [(far_codes[e][s][:, cols], far_scales[e][4 * s :, cols]) for s in range(PASSES)])
+                first_bank(e, f"hf{e}{g}", hidden[:, 512 * g : 512 * (g + 1)], [(far_codes[e][0][s][:, cols], far_codes[e][1][4 * s :, cols]) for s in range(PASSES)])
             nc.vector.quantize_mx(out=hf_codes[e][:].bitcast(FP8X4), scales=hf_scales[e][:], in_=hidden[:])
 
         def first_own(e):
             hidden = take("ho")
             a, b = divmod(e, E // OWN_PARTS)
             cols = slice(C * b, C * (b + 1))
-            first_bank(e, f"ho{e}", hidden[:], [(own_codes[s][a][:, cols], own_scales[s][a][:, cols]) for s in range(PASSES)])
+            first_bank(e, f"ho{e}", hidden[:], [(own_codes[a][s][0][:, cols], own_codes[a][s][1][:, cols]) for s in range(PASSES)])
             nc.vector.quantize_mx(out=ho_codes[e][:].bitcast(FP8X4), scales=ho_scales[e][:], in_=hidden[:])
 
         def second_matmul(e, c, dst, codes, scales):
@@ -234,7 +236,7 @@ def tile_moe_loc_mlp_relu_kernel(tc, x_words, x_scales, xo, w1, w2, gate, offs, 
         def second_own(e):
             scattered.append(e)
             slots = slice(C * e, C * (e + 1))
-            for tiles in ([(0, 1), (2, 3)] if e in SPLIT else [(0, 1, 2, 3)]):
+            for tiles in ([(0, 1), (2, 3)] if e in SPLIT + Y_SPLIT else [(0, 1, 2, 3)]):
                 n = len(tiles)
                 bank = take("ob")[:, : n * C].rearrange("p (i m) -> p i m", i=n)
                 for i, c in enumerate(tiles):

@@ -18,14 +18,16 @@ ADD = mybir.AluOpType.add
 
 P = 128
 PASSES = K // 512
-LOADS = ["xw1","l2","xo00","sc","xo01","l1","xo10","w101","w100","xo11","xw0","w111","w20","w121","w21","w120","w110","w131","gate","w130","w22","w230","w231"]
-WHO = {"w231":"V","w130":"V","w111":"C","w120":"A","ho0":"V","w121":"C","w110":"C","hf00":"V","hf01":"V"}
-STEPS = [["cx",0,1],["cx",0,0],["p1",0,0],["p1",2,1],["cx",1,0],["p1",0,1],["p1",2,0],["cx",1,1],["go",3],["p1",1,1],["p2",1],["gf",0],["go",1],["go",0],["f1",0],["p1",1,0],["gf",1],["p2",0],["gf",2],["go",2],["p1",3,0],["o1",1],["o1",0],["o2",0],["p1",3,1],["f1",1],["p2",3],["o2",1],["p2",2],["f1",2],["gf",3],["f2",0],["o1",2],["o1",3],["f1",3],["o2",2],["f2",3],["f2",1],["f2",2],["o2",3]]
+LOADS = ["xw1","l2","sc","xo00","w100","l1","xo01","xw0","w101","xo10","xo11","w121","w110","w20","w111","w120","gate","w21","w131","w130","w22","w230","w231"]
+WHO = {"w230":"B","w231":"A","w121":"A","ho1":"V","w130":"V","w111":"C","w110":"C","ho0":"V","w120":"V","w131":"B"}
+STEPS = [["cx",0,0],["cx",1,0],["cx",0,1],["cx",1,1],["p2",0],["go",0],["p1",0,0],["p1",0,1],["gf",0],["go",1],["gf",1],["p1",1,1],["p1",3,0],["f1",0],["p1",2,1],["p1",1,0],["p1",2,0],["o1",1],["f1",2],["o1",0],["f1",1],["o1",2],["o2",0],["p2",1],["f2",0],["p1",3,1],["f1",3],["p2",3],["o2",1],["f2",1],["p2",2],["o1",3],["o2",2],["f2",2],["f2",3],["o2",3]]
 SPLIT = [3]
-BUFS = {"raw":7,"w":5,"hb":4,"ob":4,"hf":3,"ho":3,"sums":2,"fc":4,"oc":4,"og":4}
-Y_SPLIT = [0,1,2]
-OWN_PARTS = 4
-GATE_IN_SCATTER = False
+BUFS = {"raw":8,"w":6,"hb":5,"ob":3,"hf":2,"ho":2,"sums":3,"fc":3,"oc":4,"og":4}
+Y_SPLIT = [2]
+ALIAS = {"ho":"ho","sums":"sums","hf":"hf"}
+FAR_PARTS = 2
+OWN_PARTS = 2
+GATE_IN_SCATTER = True
 
 
 def tile_moe_loc_mlp_relu_kernel(tc, x_words, x_scales, xo, w1, w2, gate, offs, offs2, out):
@@ -49,13 +51,14 @@ def tile_moe_loc_mlp_relu_kernel(tc, x_words, x_scales, xo, w1, w2, gate, offs, 
             "sums": [held([P, 4 * C], F32, f"sums{i}") for i in range(BUFS["sums"])],
             "og": [[held([P, 4 * T // OWN_PARTS], BF16, f"own_bf{i}{s}") for s in range(PASSES)] for i in range(min(BUFS["og"], OWN_PARTS))],
             "oc": [[(held([P, T // OWN_PARTS], U32, f"own_codes{i}{s}"), held([P, T // OWN_PARTS], U8, f"own_scales{i}{s}")) for s in range(PASSES)] for i in range(min(BUFS["oc"], OWN_PARTS))],
-            "fc": [([held([P, D], U32, f"far_codes{i}{s}") for s in range(PASSES)], held([P, D], U8, f"far_scales{i}")) for i in range(BUFS["fc"])],
+            "fc": [([held([P, E * D // FAR_PARTS], U32, f"far_codes{i}{s}") for s in range(PASSES)], held([P, E * D // FAR_PARTS], U8, f"far_scales{i}")) for i in range(min(BUFS["fc"], FAR_PARTS))],
             "hb": [psum.tile([P, 512], F32, name=f"h_bank{i}") for i in range(BUFS["hb"])],
             "ob": [psum.tile([P, 512], F32, name=f"o_bank{i}") for i in range(BUFS["ob"])],
         }
         taken = {name: 0 for name in rings}
 
         def take(name):
+            name = ALIAS.get(name, name)
             taken[name] += 1
             return rings[name][(taken[name] - 1) % BUFS[name]]
 
@@ -151,7 +154,7 @@ def tile_moe_loc_mlp_relu_kernel(tc, x_words, x_scales, xo, w1, w2, gate, offs, 
 
         def gather_far(e):
             far_codes[e] = take("fc")
-            slots = far_list[:, 16 * e : 16 * (e + 1)]
+            slots = far_list[:, 64 // FAR_PARTS * e : 64 // FAR_PARTS * (e + 1)]
             nc.vector.tensor_copy(far_codes[e][0][0][:], far_words[0][:].bitcast(U32).indirect(slots))
             nc.vector.tensor_copy(far_codes[e][1][:], far_bytes[:].bitcast(U8).indirect(slots))
             nc.vector.tensor_copy(far_codes[e][0][1][:], far_words[1][:].bitcast(U32).indirect(slots))
@@ -196,18 +199,19 @@ def tile_moe_loc_mlp_relu_kernel(tc, x_words, x_scales, xo, w1, w2, gate, offs, 
                 nc.vector.tensor_scalar_max(out=dst, in0=src, scalar1=0.0)
 
         def first_far(e):
-            hidden = take("hf")
+            hidden = take("hf")[:, : 4 * D]
             for g in range(2):
-                cols = slice(P * g, P * (g + 1))
-                first_bank(e, f"hf{e}{g}", hidden[:, 512 * g : 512 * (g + 1)], [(far_codes[e][0][s][:, cols], far_codes[e][1][4 * s :, cols]) for s in range(PASSES)])
-            nc.vector.quantize_mx(out=hf_codes[e][:].bitcast(FP8X4), scales=hf_scales[e][:], in_=hidden[:])
+                a, b = divmod(e, E // FAR_PARTS)
+                cols = slice(D * b + P * g, D * b + P * (g + 1))
+                first_bank(e, f"hf{e}{g}", hidden[:, 512 * g : 512 * (g + 1)], [(far_codes[a][0][s][:, cols], far_codes[a][1][4 * s :, cols]) for s in range(PASSES)])
+            nc.vector.quantize_mx(out=hf_codes[e][:].bitcast(FP8X4), scales=hf_scales[e][:], in_=hidden)
 
         def first_own(e):
-            hidden = take("ho")
+            hidden = take("ho")[:, : 4 * C]
             a, b = divmod(e, E // OWN_PARTS)
             cols = slice(C * b, C * (b + 1))
-            first_bank(e, f"ho{e}", hidden[:], [(own_codes[a][s][0][:, cols], own_codes[a][s][1][:, cols]) for s in range(PASSES)])
-            nc.vector.quantize_mx(out=ho_codes[e][:].bitcast(FP8X4), scales=ho_scales[e][:], in_=hidden[:])
+            first_bank(e, f"ho{e}", hidden, [(own_codes[a][s][0][:, cols], own_codes[a][s][1][:, cols]) for s in range(PASSES)])
+            nc.vector.quantize_mx(out=ho_codes[e][:].bitcast(FP8X4), scales=ho_scales[e][:], in_=hidden)
 
         def second_matmul(e, c, dst, codes, scales):
             nc.tensor.matmul_mx(

from contextlib import ExitStack

import concourse.mybir as mybir

K, T, Q, E, C, D, H, N = 1024, 512, 1024, 4, 128, 256, 512, 512
FLOPS = 2 * E * (C + D) * (K * H + H * N)

F32 = mybir.dt.float32
BF16 = mybir.dt.bfloat16
I32 = mybir.dt.int32
U32 = mybir.dt.uint32
U16 = mybir.dt.uint16
U8 = mybir.dt.uint8
FP8X4 = mybir.dt.float8_e4m3fn_x4
RELU = mybir.ActivationFunctionType.Relu
MULT = mybir.AluOpType.mult
ADD = mybir.AluOpType.add

P = 128
PASSES = K // 512
LOADS = ["xw1","l2","sc","xo00","w100","l1","xo01","xw0","w101","xo10","xo11","w121","w110","w20","w111","w120","gate","w21","w131","w130","w22","w230","w231"]
WHO = {"w230":"B","w231":"A","w121":"A","ho1":"V","w130":"V","w111":"C","w110":"C","ho0":"V","w120":"V","w131":"B"}
STEPS = [["cx",0,0],["cx",1,0],["cx",0,1],["cx",1,1],["p2",0],["go",0],["p1",0,0],["p1",0,1],["gf",0],["go",1],["gf",1],["p1",1,1],["p1",3,0],["f1",0],["p1",2,1],["p1",1,0],["p1",2,0],["o1",1],["f1",2],["o1",0],["f1",1],["o1",2],["o2",0],["p2",1],["f2",0],["p1",3,1],["f1",3],["p2",3],["o2",1],["f2",1],["p2",2],["o1",3],["o2",2],["f2",2],["f2",3],["o2",3]]
SPLIT = [3]
BUFS = {"raw":8,"w":6,"hb":5,"ob":3,"hf":2,"ho":2,"sums":3,"fc":3,"oc":4,"og":4}
Y_SPLIT = [2]
ALIAS = {"ho":"ho","sums":"sums","hf":"hf"}
FAR_PARTS = 2
OWN_PARTS = 2
GATE_IN_SCATTER = True


def tile_moe_loc_mlp_relu_kernel(tc, x_words, x_scales, xo, w1, w2, gate, offs, offs2, out):
    nc = tc.nc
    with ExitStack() as ctx:
        keep = ctx.enter_context(tc.tile_pool(name="keep", bufs=1))
        psum = ctx.enter_context(tc.psum_pool(name="psum", bufs=1))

        def held(shape, dtype, name):
            return keep.tile(shape, dtype, name=name, align_bytes=64)

        own_list = held([P, T // 16], U16, "own_list")
        far_list = held([P, E * D // 16], U16, "far_list")
        far_words = [held([P, Q], I32, f"far_words{s}") for s in range(PASSES)]
        far_bytes = held([P, Q // 4], I32, "far_bytes")
        rings = {
            "raw": [held([P, 4 * H], F32, f"raw{i}") for i in range(BUFS["raw"])],
            "w": [held([P, 4 * H], BF16, f"w_bf{i}") for i in range(BUFS["w"])],
            "hf": [held([P, 4 * D], BF16, f"hidden_far{i}") for i in range(BUFS["hf"])],
            "ho": [held([P, 4 * C], BF16, f"hidden_own{i}") for i in range(BUFS["ho"])],
            "sums": [held([P, 4 * C], F32, f"sums{i}") for i in range(BUFS["sums"])],
            "og": [[held([P, 4 * T // OWN_PARTS], BF16, f"own_bf{i}{s}") for s in range(PASSES)] for i in range(min(BUFS["og"], OWN_PARTS))],
            "oc": [[(held([P, T // OWN_PARTS], U32, f"own_codes{i}{s}"), held([P, T // OWN_PARTS], U8, f"own_scales{i}{s}")) for s in range(PASSES)] for i in range(min(BUFS["oc"], OWN_PARTS))],
            "fc": [([held([P, E * D // FAR_PARTS], U32, f"far_codes{i}{s}") for s in range(PASSES)], held([P, E * D // FAR_PARTS], U8, f"far_scales{i}")) for i in range(min(BUFS["fc"], FAR_PARTS))],
            "hb": [psum.tile([P, 512], F32, name=f"h_bank{i}") for i in range(BUFS["hb"])],
            "ob": [psum.tile([P, 512], F32, name=f"o_bank{i}") for i in range(BUFS["ob"])],
        }
        taken = {name: 0 for name in rings}

        def take(name):
            name = ALIAS.get(name, name)
            taken[name] += 1
            return rings[name][(taken[name] - 1) % BUFS[name]]

        w_raw = {}
        pending = list(LOADS)
        staged = []
        rounded = set()
        gates = held([P, E * C], F32, "gates")

        nc.gpsimd.memset(far_bytes[:], 0)
        scale_rows = x_scales.bitcast(I32)

        def load(name):
            if name == "sc":
                for q in range(4):
                    nc.sync.dma_start(out=far_bytes[32 * q : 32 * q + 8, :], in_=scale_rows[:, 4 * q : 4 * q + 4, :])
            elif name == "l1":
                nc.sync.dma_start(own_list[:], offs)
            elif name == "l2":
                nc.sync.dma_start(far_list[:], offs2)
            elif name == "gate":
                nc.sync.dma_start(out=gates[:], in_=gate)
            elif name.startswith("xw"):
                s = int(name[2])
                nc.sync.dma_start(out=far_words[s][:], in_=x_words[s].rearrange("p t d -> p (t d)").bitcast(I32))
            else:
                if name.startswith("xo"):
                    s, u = int(name[2]), int(name[3])
                    rows = xo[512 * s : 512 * (s + 1), :].rearrange("(p j) t -> p j t", j=4)[:, 2 * u : 2 * u + 2, :]
                elif name.startswith("w1"):
                    e, s = int(name[2]), int(name[3])
                    rows = w1[e, 512 * s : 512 * (s + 1), :].rearrange("(p j) c -> p j c", j=4)
                elif len(name) == 3:
                    rows = w2[int(name[2])].rearrange("(p j) n -> p j n", j=4)
                else:
                    h = int(name[3])
                    rows = w2[int(name[2])][:, 256 * h : 256 * (h + 1)].rearrange("(p j) n -> p j n", j=4)
                j, width = rows.shape[1], rows.shape[2]
                w_raw[name] = take("raw")[:, : j * width].rearrange("p (j c) -> p j c", j=j)
                nc.sync.dma_start(out=w_raw[name], in_=rows)

        def load_ahead():
            while pending:
                name = pending[0]
                if name[0] == "w" or name.startswith("xo"):
                    if len(staged) >= BUFS["raw"] and staged[-BUFS["raw"]] not in rounded:
                        return
                    staged.append(name)
                load(pending.pop(0))

        xo_pairs = [[held([P, T, 2], BF16, f"xo_pairs{s}{u}") for u in range(2)] for s in range(PASSES)]
        own_codes, far_codes = {}, {}
        w1_codes = [[held([P, H], U32, f"w1_codes{e}{s}") for s in range(PASSES)] for e in range(E)]
        w1_scales = [[held([P, H], U8, f"w1_scales{e}{s}") for s in range(PASSES)] for e in range(E)]
        w2_codes = [held([P, N], U32, f"w2_codes{e}") for e in range(E)]
        w2_scales = [held([P, N], U8, f"w2_scales{e}") for e in range(E)]
        hf_codes = [held([P, D], U32, f"hf_codes{e}") for e in range(E)]
        hf_scales = [held([P, D], U8, f"hf_scales{e}") for e in range(E)]
        ho_codes = [held([P, C], U32, f"ho_codes{e}") for e in range(E)]
        ho_scales = [held([P, C], U8, f"ho_scales{e}") for e in range(E)]
        own_out = [held([P, T], F32, f"own_out{c}") for c in range(4)]
        far_out = [held([P, 4, D], F32, f"far_out{e}") for e in range(E)]
        scattered = []

        def cast(name, dst, src):
            who = WHO.get(name, "S")
            rounded.add(name)
            half = dst.shape[1] * {"A": 1, "C": 3}.get(who, 2) // 4
            if who == "S":
                nc.scalar.copy(out=dst, in_=src)
            elif who == "V":
                nc.vector.tensor_copy(out=dst, in_=src)
            elif who == "G":
                for a in range(4):
                    part = slice(a * half // 2, (a + 1) * half // 2)
                    nc.gpsimd.tensor_scalar(out=dst[:, part], in0=src[:, part], scalar1=1.0, scalar2=0.0, op0=MULT, op1=ADD)
            else:
                nc.scalar.copy(out=dst[:, :half], in_=src[:, :half])
                nc.vector.tensor_copy(out=dst[:, half:], in_=src[:, half:])

        def cast_xo(s, u):
            cast(f"xo{s}{u}", xo_pairs[s][u][:], w_raw[f"xo{s}{u}"].rearrange("p r t -> p t r"))

        def gather_own(a):
            own_bf, own_codes[a] = take("og"), take("oc")
            for s in range(PASSES):
                words = own_bf[s][:].bitcast(U32).rearrange("p (n u) -> p n u", u=2)
                for u in range(2):
                    window = xo_pairs[s][u][:].rearrange("p t r -> p (t r)").bitcast(U32)
                    nc.vector.tensor_copy(words[:, :, u], window.indirect(own_list[:, 32 // OWN_PARTS * a : 32 // OWN_PARTS * (a + 1)]))
            for s in range(PASSES):
                nc.vector.quantize_mx(out=own_codes[a][s][0][:].bitcast(FP8X4), scales=own_codes[a][s][1][:], in_=own_bf[s][:])

        def gather_far(e):
            far_codes[e] = take("fc")
            slots = far_list[:, 64 // FAR_PARTS * e : 64 // FAR_PARTS * (e + 1)]
            nc.vector.tensor_copy(far_codes[e][0][0][:], far_words[0][:].bitcast(U32).indirect(slots))
            nc.vector.tensor_copy(far_codes[e][1][:], far_bytes[:].bitcast(U8).indirect(slots))
            nc.vector.tensor_copy(far_codes[e][0][1][:], far_words[1][:].bitcast(U32).indirect(slots))

        def prepare_w1(e, s):
            grouped = take("w")
            cast(
                f"w1{e}{s}",
                grouped[:].rearrange("p (t m j) -> p m j t", t=4, j=4),
                w_raw[f"w1{e}{s}"].rearrange("p j (m t) -> p m j t", t=4),
            )
            nc.vector.quantize_mx(out=w1_codes[e][s][:].bitcast(FP8X4), scales=w1_scales[e][s][:], in_=grouped[:])

        def prepare_w2(e):
            parts = [(f"w2{e}{h}", slice(256 * h, 256 * (h + 1)), 256) for h in range(2)] if e in SPLIT else [(f"w2{e}", slice(0, N), N)]
            for name, cols, width in parts:
                grouped = take("w")[:, : 4 * width]
                cast(
                    name,
                    grouped.rearrange("p (c i j) -> p c j i", i=4, j=4),
                    w_raw[name].rearrange("p j (c i) -> p c j i", i=4),
                )
                nc.vector.quantize_mx(out=w2_codes[e][:, cols].bitcast(FP8X4), scales=w2_scales[e][:, cols], in_=grouped)

        def first_bank(e, name, hidden, operands):
            bank = take("hb")[:].rearrange("p (t n) -> p t n", t=4)
            for t in range(4):
                for s in range(PASSES):
                    nc.tensor.matmul_mx(
                        out=bank[:, t, :],
                        lhsT=w1_codes[e][s][:, P * t : P * (t + 1)].bitcast(FP8X4),
                        lhsT_scale=w1_scales[e][s][:, P * t : P * (t + 1)],
                        rhs=operands[s][0].bitcast(FP8X4),
                        rhs_scale=operands[s][1],
                        start=(s == 0),
                        stop=(s == PASSES - 1),
                    )
            dst, src = hidden.rearrange("p (n t) -> p n t", t=4), bank.rearrange("p t n -> p n t")
            if WHO.get(name, "S") == "S":
                nc.scalar.activation(out=dst, in_=src, func=RELU)
            else:
                nc.vector.tensor_scalar_max(out=dst, in0=src, scalar1=0.0)

        def first_far(e):
            hidden = take("hf")[:, : 4 * D]
            for g in range(2):
                a, b = divmod(e, E // FAR_PARTS)
                cols = slice(D * b + P * g, D * b + P * (g + 1))
                first_bank(e, f"hf{e}{g}", hidden[:, 512 * g : 512 * (g + 1)], [(far_codes[a][0][s][:, cols], far_codes[a][1][4 * s :, cols]) for s in range(PASSES)])
            nc.vector.quantize_mx(out=hf_codes[e][:].bitcast(FP8X4), scales=hf_scales[e][:], in_=hidden)

        def first_own(e):
            hidden = take("ho")[:, : 4 * C]
            a, b = divmod(e, E // OWN_PARTS)
            cols = slice(C * b, C * (b + 1))
            first_bank(e, f"ho{e}", hidden, [(own_codes[a][s][0][:, cols], own_codes[a][s][1][:, cols]) for s in range(PASSES)])
            nc.vector.quantize_mx(out=ho_codes[e][:].bitcast(FP8X4), scales=ho_scales[e][:], in_=hidden)

        def second_matmul(e, c, dst, codes, scales):
            nc.tensor.matmul_mx(
                out=dst,
                lhsT=w2_codes[e][:, P * c : P * (c + 1)].bitcast(FP8X4),
                lhsT_scale=w2_scales[e][:, P * c : P * (c + 1)],
                rhs=codes[:].bitcast(FP8X4),
                rhs_scale=scales[:],
                start=True,
                stop=True,
            )

        def second_far(e):
            for b in range(2):
                far_bank = take("ob")[:].rearrange("p (i m) -> p i m", i=2)
                for i in range(2):
                    second_matmul(e, 2 * b + i, far_bank[:, i, :], hf_codes[e], hf_scales[e])
                if WHO.get(f"zf{e}{b}", "S") == "S":
                    nc.scalar.copy(out=far_out[e][:, 2 * b : 2 * b + 2, :], in_=far_bank)
                else:
                    nc.vector.tensor_copy(out=far_out[e][:, 2 * b : 2 * b + 2, :], in_=far_bank)
            nc.sync.dma_start(
                out=out[:, T + D * e : T + D * (e + 1)].rearrange("(c p) m -> p c m", p=P), in_=far_out[e][:]
            )

        def second_own(e):
            scattered.append(e)
            slots = slice(C * e, C * (e + 1))
            for tiles in ([(0, 1), (2, 3)] if e in SPLIT + Y_SPLIT else [(0, 1, 2, 3)]):
                n = len(tiles)
                bank = take("ob")[:, : n * C].rearrange("p (i m) -> p i m", i=n)
                for i, c in enumerate(tiles):
                    second_matmul(e, c, bank[:, i, :], ho_codes[e], ho_scales[e])
                sums = take("sums")[:, : n * C].rearrange("p (i m) -> p i m", i=n)
                if GATE_IN_SCATTER:
                    nc.scalar.copy(out=sums, in_=bank)
                else:
                    nc.vector.tensor_tensor(out=sums, in0=bank, in1=gates[:, slots].unsqueeze(1).broadcast_to([P, n, C]), op=MULT)
                for i, c in enumerate(tiles):
                    window = own_out[c][:].indirect(own_list[:, 8 * e : 8 * (e + 1)])
                    if GATE_IN_SCATTER:
                        nc.vector.tensor_tensor(window, sums[:, i, :], gates[:, slots], MULT)
                    else:
                        nc.vector.tensor_copy(window, sums[:, i, :])
                    if len(scattered) == E:
                        nc.sync.dma_start(out=out[P * c : P * (c + 1), 0:T], in_=own_out[c][:])

        steps = {"cx": cast_xo, "gf": gather_far, "go": gather_own, "p1": prepare_w1, "p2": prepare_w2, "f1": first_far, "o1": first_own, "f2": second_far, "o2": second_own}
        load_ahead()
        for step in STEPS:
            steps[step[0]](*step[1:])
            load_ahead()
